import numpy as np
import ml_dtypes


def mxq(x, axis, fmt="e4m3"):
    dtype, down = {"e4m3": (ml_dtypes.float8_e4m3fn, 7), "e5m2": (ml_dtypes.float8_e5m2, 14)}[fmt]
    v = np.moveaxis(np.asarray(x, np.float32).astype(ml_dtypes.bfloat16).astype(np.float64), axis, -1)
    blocks = v.reshape(v.shape[:-1] + (-1, 32))
    amax = np.abs(blocks).max(-1, keepdims=True)
    byte = np.maximum(np.where(amax > 0, np.frexp(amax)[1] - 1 + 127, 0) - down, 1)
    scale = np.exp2(byte - 127.0)
    codes = (blocks / scale).astype(np.float32).astype(dtype).astype(np.float64)
    return np.moveaxis((codes * scale).reshape(v.shape), -1, axis)


WIDE = False


def mx_kscale(k):
    if not WIDE:
        return np.ones(k)
    levels = np.array([10, -10, 5, -5, 0])
    if k % 512:
        return np.exp2(np.random.permutation(np.resize(levels, k // 32))).repeat(32)
    a = np.empty((k // 512, 16))
    for p in range(k // 512):
        a[p, :8] = np.random.permutation(np.resize(levels, 8))
        for g in range(8):
            far = levels[np.abs(levels - a[p, g]) >= 10]
            a[p, g + 8] = far[np.random.randint(len(far))]
    return np.exp2(a.ravel()).repeat(32)


def f64(x):
    return np.asarray(x).astype(np.float64)


def striped(idx):
    return np.tile(idx.reshape(-1, 16).T, (8, 1)).astype(np.uint16)


def unstriped(offs):
    return offs[:16].T.reshape(-1).astype(np.int64)


E2M1 = np.array([0.0, 0.5, 1.0, 1.5, 2.0, 3.0, 4.0, 6.0, -0.0, -0.5, -1.0, -1.5, -2.0, -3.0, -4.0, -6.0])


def pack_weight(w, fmt):
    k, n = w.shape
    w = f64(np.asarray(w, np.float32).astype(ml_dtypes.bfloat16)).reshape(k // 32, 32, n)
    amax = np.abs(w).max(1)
    if fmt == "e4m3":
        byte = np.frexp(amax)[1] - 1 + 127 - 7
    else:
        mant, ex = np.frexp(amax / 6.0)
        byte = np.where(mant > 0.5, ex, ex - 1) + 127
    byte = np.clip(np.where(amax > 0, byte, 1), 1, 254)
    scaled = (w * np.exp2(127.0 - byte)[:, None, :]).reshape(k, n).astype(np.float32)
    by_word = np.ascontiguousarray(scaled.reshape(k // 512, 128, 4, n).transpose(0, 1, 3, 2))
    if fmt == "e4m3":
        words = by_word.astype(ml_dtypes.float8_e4m3fn).view(np.uint8)
    else:
        c = by_word.astype(ml_dtypes.float4_e2m1fn).view(np.uint8) & 0xF
        words = (c[..., 0::2] | (c[..., 1::2] << 4)).reshape(k // 512, 128, 2 * n)
    return np.ascontiguousarray(words), np.ascontiguousarray(byte.astype(np.uint8).reshape(k // 512, 16, n))


def unpack_weight(words, scales, fmt):
    g, _, n = scales.shape
    words = np.ascontiguousarray(words).reshape(g, 128, n, -1)
    if fmt == "e4m3":
        vals = words.view(ml_dtypes.float8_e4m3fn).astype(np.float64)
    else:
        nib = np.empty((g, 128, n, 4), np.uint8)
        nib[..., 0::2] = words & 0xF
        nib[..., 1::2] = words >> 4
        vals = E2M1[nib]
    vals = vals * np.repeat(np.exp2(scales.astype(np.float64) - 127.0), 8, axis=1)[..., None]
    return vals.transpose(0, 1, 3, 2).reshape(g * 512, n)


def gelu(v):
    return 0.5 * v * (1.0 + np.tanh(np.sqrt(2.0 / np.pi) * (v + 0.044715 * v**3)))


K, T, S, H, N = 1024, 4096, 512, 1536, 512

def setup_inputs():
    n = np.random.standard_normal
    s = mx_kscale(K)[:, None]
    u = mx_kscale(H)[:, None]
    tab_words, tab_scales = pack_weight(n((K, T)) * s, "e4m3")
    w2_words, w2_scales = pack_weight(0.85 * n((K, H)) / np.sqrt(K) / s, "e2m1")
    w4_words, w4_scales = pack_weight(n((H, N)) / np.sqrt(H) / u, "e4m3")
    return {
        "tab_words": tab_words, "tab_scales": tab_scales,
        "offs": striped(np.random.permutation(T)[:S]),
        "offs2": striped(np.random.permutation(T)[:S]),
        "offs3": striped(np.random.permutation(T)[:S]),
        "w1": (0.85 * n((K, H)) / np.sqrt(K) / s).astype(np.float32),
        "w2_words": w2_words, "w2_scales": w2_scales,
        "w3": (0.85 * n((K, H)) / np.sqrt(K) / s).astype(np.float32),
        "bias": (0.5 * n(H)).astype(np.float32),
        "profile": n((H, S)).astype(np.float32),
        "gain": (np.exp(0.3 * n(H)) * u[:, 0]).astype(np.float32),
        "w4_words": w4_words, "w4_scales": w4_scales,
    }

def reference(tab_words, tab_scales, offs, offs2, offs3, w1, w2_words, w2_scales, w3,
              bias, profile, gain, w4_words, w4_scales):
    TW = unpack_weight(tab_words, tab_scales, "e4m3")
    v = TW[:, unstriped(offs)]
    v2 = TW[:, unstriped(offs2)]
    v3 = TW[:, unstriped(offs3)]
    w1q = mxq(f64(w1), 0, "e4m3")
    w2q = unpack_weight(w2_words, w2_scales, "e2m1")
    w3q = mxq(f64(w3), 0, "e4m3")
    w4q = unpack_weight(w4_words, w4_scales, "e4m3")
    total = (w1q.T @ v + w2q.T @ v2 + w3q.T @ v3) + f64(bias)[:, None]
    h = f64(gain)[:, None] * (np.tanh(total) * f64(profile) + total)
    hq = mxq(h, 0, "e4m3")
    return w4q.T @ hq

@@ -1,0 +1,256 @@
+from contextlib import ExitStack
+
+import concourse.mybir as mybir
+
+K, T, S, H, N = 1024, 4096, 512, 1536, 512
+FLOPS = 2 * (3 * K * H * S + H * N * S)
+
+F32 = mybir.dt.float32
+BF16 = mybir.dt.bfloat16
+I32 = mybir.dt.int32
+U32 = mybir.dt.uint32
+U16 = mybir.dt.uint16
+U8 = mybir.dt.uint8
+FP8X4 = mybir.dt.float8_e4m3fn_x4
+FP4X4 = mybir.dt.float4_e2m1fn_x4
+ACT = mybir.ActivationFunctionType
+ALU = mybir.AluOpType
+
+P = 128
+PACK = 4
+KP = P * PACK
+PASSES = K // KP
+BLOCKS = H // KP
+HALF = S // 2
+TAB_ROW = 4
+W4_ROW = 12
+
+
+def tile_list_preposition_slot_scores_kernel(
+    tc, tab_words, tab_scales, offs, offs2, offs3, w1, w2_words, w2_scales, w3,
+    bias, profile, gain, w4_words, w4_scales, out,
+):
+    nc = tc.nc
+    with ExitStack() as ctx:
+        held = ctx.enter_context(tc.tile_pool(name="held", bufs=1))
+        ring = ctx.enter_context(tc.tile_pool(name="ring", bufs=1))
+        psum = ctx.enter_context(tc.psum_pool(name="psum", bufs=1))
+
+        lists = [held.tile([P, S // 16], U16, name="list%d" % i) for i in range(3)]
+        table = [held.tile([P, T], I32, name="table%d" % a, align_bytes=64) for a in range(PASSES)]
+        tab_plane = held.tile([P, T], U8, align_bytes=64)
+        picked = [[held.tile([P, S], U32, name="picked%d_%d" % (i, a), align_bytes=64) for a in range(PASSES)]
+                  for i in range(3)]
+        picked_plane = [held.tile([P, S], U8, name="pplane%d" % i, align_bytes=64) for i in range(3)]
+        lowered = [held.tile([P, S], U8, name="lowered%d" % a, align_bytes=64) for a in range(PASSES)]
+        w2_raw = held.tile([P, PASSES * 2 * H], U8, align_bytes=64)
+        w2_codes = held.tile([P, PASSES * 2 * H], U8, align_bytes=64)
+        w2_plane_raw = held.tile([P, PASSES * H], U8, align_bytes=64)
+        w2_plane = held.tile([P, PASSES * H], U8, align_bytes=64)
+        w4_codes = held.tile([P, BLOCKS * N], I32, align_bytes=64)
+        w4_plane = held.tile([P, BLOCKS * N], U8, align_bytes=64)
+        bias_sb = held.tile([P, BLOCKS, PACK], F32)
+        gain_sb = held.tile([P, BLOCKS, PACK], F32)
+        gain_bias = held.tile([P, BLOCKS, PACK], F32)
+        prof = [held.tile([P, PACK, S], F32, name="prof%d" % b) for b in range(BLOCKS)]
+
+        for plane in (w2_plane_raw, tab_plane, lowered[0], lowered[1], w4_plane):
+            nc.vector.memset(plane[:].bitcast(I32), 0)
+
+        for q in range(4):
+            r0 = 32 * q + TAB_ROW
+            nc.gpsimd.dma_start(out=tab_plane[r0:r0 + 4 * PASSES, :].bitcast(I32),
+                                in_=tab_scales[:, 4 * q:4 * q + 4, :].bitcast(I32))
+
+        weights = {0: w1, 2: w3}
+        raw, quant, total, hq = {}, {}, {}, {}
+
+        def load_table(a):
+            nc.sync.dma_start(out=table[a][:], in_=tab_words[a].rearrange("p n i -> p (n i)").bitcast(I32))
+
+        def load_chunk(key):
+            b, a, i = key
+            raw[key] = ring.tile([P, PACK, KP], F32, name="raw", bufs=6)
+            rows = weights[i][a * KP:(a + 1) * KP, b * KP:(b + 1) * KP]
+            nc.sync.dma_start(out=raw[key][:], in_=rows.rearrange("(p j) c -> p j c", j=PACK))
+
+        def load_profile(b):
+            nc.sync.dma_start(out=prof[b][:],
+                              in_=profile[b * KP:(b + 1) * KP, :].rearrange("(p t) s -> p t s", t=PACK))
+
+        def gather_words(a):
+            for i in range(3):
+                nc.vector.tensor_copy(picked[i][a][:], table[a][:].bitcast(U32).indirect(lists[i][:]))
+
+        def quantize_chunk(key, on_vector):
+            grouped = ring.tile([P, PACK * P * PACK], BF16, name="grouped", bufs=3, align_bytes=64)
+            dst = grouped[:].rearrange("p (t m j) -> p m j t", t=PACK, j=PACK)
+            src = raw[key][:].rearrange("p j (m t) -> p m j t", t=PACK)
+            if on_vector:
+                nc.vector.tensor_copy(out=dst, in_=src)
+            else:
+                nc.scalar.copy(out=dst, in_=src)
+            codes = ring.tile([P, KP], U32, name="codes", bufs=8, align_bytes=64)
+            plane = ring.tile([P, KP], U8, name="plane", bufs=8, align_bytes=64)
+            nc.vector.quantize_mx(out=codes[:].bitcast(FP8X4), scales=plane[:], in_=grouped[:])
+            quant[key] = (codes, plane)
+
+        def multiply(key, first, last):
+            b, a, i = key
+            if first:
+                total[b] = [psum.tile([P, S], F32, name="bank%d" % (4 * (b % 2) + t)) for t in range(PACK)]
+            for t in range(PACK):
+                if i == 1:
+                    c0 = a * H + b * KP + t * P
+                    lhs = w2_codes[:, 2 * c0:2 * (c0 + P)].bitcast(FP4X4)
+                    lhs_scale = w2_plane[:, c0:c0 + P]
+                    rhs_scale = lowered[a][:]
+                else:
+                    codes, plane = quant[key]
+                    lhs = codes[:, t * P:(t + 1) * P].bitcast(FP8X4)
+                    lhs_scale = plane[:, t * P:(t + 1) * P]
+                    rhs_scale = picked_plane[i][TAB_ROW + 4 * a:P, :]
+                nc.tensor.matmul_mx(out=total[b][t][:], lhsT=lhs, lhsT_scale=lhs_scale,
+                                    rhs=picked[i][a][:].bitcast(FP8X4), rhs_scale=rhs_scale,
+                                    start=first, stop=last)
+
+        def epilogue(b, s0, width):
+            cols = slice(s0, s0 + width)
+            bent = ring.tile([P, PACK, width], F32, name="bent", bufs=2)
+            straight = ring.tile([P, PACK, width], F32, name="straight", bufs=2)
+            for t in range(PACK):
+                nc.scalar.activation(out=bent[:, t, :], in_=total[b][t][:, cols], func=ACT.Tanh,
+                                     bias=bias_sb[:, b, t:t + 1])
+                nc.scalar.activation(out=straight[:, t, :], in_=total[b][t][:, cols], func=ACT.Identity,
+                                     bias=gain_bias[:, b, t:t + 1], scale=gain_sb[:, b, t:t + 1])
+            for t in range(PACK):
+                nc.vector.scalar_tensor_tensor(out=bent[:, t, :], in0=bent[:, t, :], scalar=gain_sb[:, b, t:t + 1],
+                                               in1=prof[b][:, t, cols], op0=ALU.mult, op1=ALU.mult)
+            h = ring.tile([P, width * PACK], BF16, name="h", bufs=2, align_bytes=64)
+            nc.vector.tensor_tensor(out=h[:].rearrange("p (c i t) -> p c t i", i=4, t=PACK),
+                                    in0=bent[:].rearrange("p t (c i) -> p c t i", i=4),
+                                    in1=straight[:].rearrange("p t (c i) -> p c t i", i=4), op=ALU.add)
+            codes = held.tile([P, width], U32, name="hc%d_%d" % (b, s0), align_bytes=64)
+            plane = held.tile([P, width], U8, name="hp%d_%d" % (b, s0), align_bytes=64)
+            nc.vector.quantize_mx(out=codes[:].bitcast(FP8X4), scales=plane[:], in_=h[:])
+            for half in range(s0 // HALF, (s0 + width) // HALF):
+                c = slice(half * HALF - s0, (half + 1) * HALF - s0)
+                hq[(b, half)] = (codes[:, c], plane[:, c])
+
+        scores = {}
+
+        def score(b, half):
+            if b == 0:
+                for pair in range(2):
+                    scores[(half, pair)] = psum.tile([P, 2, HALF], F32, name="bank%d" % (4 + 2 * half + pair))
+            codes, plane = hq[(b, half)]
+            for m in range(N // P):
+                c0 = b * N + m * P
+                nc.tensor.matmul_mx(out=scores[(half, m // 2)][:, m % 2, :],
+                                    lhsT=w4_codes[:, c0:c0 + P].bitcast(FP8X4),
+                                    lhsT_scale=w4_plane[W4_ROW:P, c0:c0 + P],
+                                    rhs=codes.bitcast(FP8X4), rhs_scale=plane,
+                                    start=(b == 0 and m % 2 == 0), stop=(b == BLOCKS - 1 and m % 2 == 1))
+
+        def store(half):
+            for pair in range(2):
+                staged = held.tile([P, 2, HALF], F32, name="staged%d_%d" % (half, pair))
+                dst = out[2 * pair * P:2 * (pair + 1) * P, half * HALF:(half + 1) * HALF]
+                dst = dst.rearrange("(m p) s -> p m s", p=P)
+                if pair == 0:
+                    nc.scalar.copy(out=staged[:], in_=scores[(half, pair)][:])
+                else:
+                    nc.vector.tensor_copy(out=staged[:], in_=scores[(half, pair)][:])
+                nc.sync.dma_start(out=dst, in_=staged[:])
+
+        chunks = [(b, a, i) for b in range(BLOCKS) for a in range(PASSES) for i in (0, 2)]
+
+        nc.sync.dma_start(out=w2_raw[:].bitcast(I32).rearrange("p (a c) -> p a c", a=PASSES),
+                          in_=w2_words.bitcast(I32).rearrange("a p c -> p a c"))
+        for q in range(4):
+            nc.sync.dma_start(
+                out=w2_plane_raw[32 * q:32 * q + 4, :].bitcast(I32).rearrange("r (a c) -> r a c", a=PASSES),
+                in_=w2_scales[:, 4 * q:4 * q + 4, :].bitcast(I32).rearrange("a r c -> r a c"))
+        load_chunk(chunks[0])
+        load_table(0)
+        for tile, src in zip(lists, (offs, offs2, offs3)):
+            nc.sync.dma_start(tile[:], src)
+        load_chunk(chunks[1])
+        load_chunk(chunks[2])
+        load_table(1)
+        for key in chunks[3:5]:
+            load_chunk(key)
+        nc.sync.dma_start(out=bias_sb[:], in_=bias.rearrange("(b p t) -> p b t", p=P, t=PACK))
+        nc.sync.dma_start(out=gain_sb[:], in_=gain.rearrange("(b p t) -> p b t", p=P, t=PACK))
+
+        nc.vector.tensor_copy(out=w2_codes[:].bitcast(U16).rearrange("p (g t m) -> p g t m", t=PACK, m=P),
+                              in_=w2_raw[:].bitcast(U16).rearrange("p (g m t) -> p g t m", t=PACK, m=P))
+        nc.vector.tensor_copy(out=w2_plane[:].rearrange("p (g t m) -> p g t m", t=PACK, m=P),
+                              in_=w2_plane_raw[:].rearrange("p (g m t) -> p g t m", t=PACK, m=P))
+        quantize_chunk(chunks[0], False)
+        for i in (1, 0, 2):
+            nc.vector.tensor_copy(picked_plane[i][:], tab_plane[:].indirect(lists[i][:]))
+        for a in range(PASSES):
+            r0 = TAB_ROW + 4 * a
+            nc.gpsimd.dma_start(out=lowered[a][0:P - 16, :].bitcast(I32),
+                                in_=picked_plane[1][r0:r0 + P - 16, :].bitcast(I32))
+        gather_words(0)
+        quantize_chunk(chunks[1], False)
+        quantize_chunk(chunks[2], False)
+        nc.vector.tensor_tensor(out=gain_bias[:], in0=gain_sb[:], in1=bias_sb[:], op=ALU.mult)
+        load_chunk(chunks[5])
+        load_chunk(chunks[6])
+        load_chunk(chunks[7])
+        load_profile(0)
+        multiply(chunks[0], True, False)
+        multiply(chunks[1], False, False)
+        gather_words(1)
+        quantize_chunk(chunks[3], False)
+        multiply((0, 0, 1), False, False)
+        multiply(chunks[2], False, False)
+        multiply((0, 1, 1), False, False)
+        multiply(chunks[3], False, True)
+
+        multiply((1, 0, 1), True, False)
+        multiply((1, 1, 1), False, False)
+        quantize_chunk(chunks[4], False)
+        load_chunk(chunks[8])
+        for q in range(4):
+            r0 = 32 * q + W4_ROW
+            nc.sync.dma_start(
+                out=w4_plane[r0:r0 + 4, :].bitcast(I32).rearrange("r (a c) -> r a c", a=BLOCKS),
+                in_=w4_scales[:, 4 * q:4 * q + 4, :].bitcast(I32).rearrange("a r c -> r a c"))
+        load_chunk(chunks[9])
+        load_profile(1)
+        multiply(chunks[4], False, False)
+        quantize_chunk(chunks[5], True)
+        load_chunk(chunks[10])
+        multiply(chunks[5], False, False)
+        quantize_chunk(chunks[6], True)
+        load_chunk(chunks[11])
+        nc.sync.dma_start(out=w4_codes[:].rearrange("p (a c) -> p a c", a=BLOCKS),
+                          in_=w4_words.rearrange("a p c i -> p a (c i)").bitcast(I32))
+        load_profile(2)
+        multiply(chunks[6], False, False)
+        quantize_chunk(chunks[7], False)
+        epilogue(0, 0, S)
+        multiply(chunks[7], False, True)
+
+        multiply((2, 0, 1), True, False)
+        multiply((2, 1, 1), False, False)
+        quantize_chunk(chunks[8], False)
+        multiply(chunks[8], False, False)
+        epilogue(1, 0, S)
+        quantize_chunk(chunks[9], True)
+        multiply(chunks[9], False, False)
+        quantize_chunk(chunks[10], False)
+        multiply(chunks[10], False, False)
+        quantize_chunk(chunks[11], True)
+        multiply(chunks[11], False, True)
+        for b in range(BLOCKS - 1):
+            for half in range(2):
+                score(b, half)
+        for half in range(2):
+            epilogue(2, half * HALF, HALF)
+            score(2, half)
+            store(half)

@@ -24,6 +24,9 @@ BLOCKS = H // KP
 HALF = S // 2
 TAB_ROW = 4
 W4_ROW = 12
+PROFILE_AFTER = (4, 10)
+STREAM_BUFS = 4
+ON_VECTOR = (5, 9, 10)
 
 
 def tile_list_preposition_slot_scores_kernel(
@@ -47,34 +50,33 @@ def tile_list_preposition_slot_scores_kernel(
         w2_codes = held.tile([P, PASSES * 2 * H], U8, align_bytes=64)
         w2_plane_raw = held.tile([P, PASSES * H], U8, align_bytes=64)
         w2_plane = held.tile([P, PASSES * H], U8, align_bytes=64)
-        w4_codes = held.tile([P, BLOCKS * N], I32, align_bytes=64)
         w4_plane = held.tile([P, BLOCKS * N], U8, align_bytes=64)
         bias_sb = held.tile([P, BLOCKS, PACK], F32)
         gain_sb = held.tile([P, BLOCKS, PACK], F32)
         gain_bias = held.tile([P, BLOCKS, PACK], F32)
-        prof = [held.tile([P, PACK, S], F32, name="prof%d" % b) for b in range(BLOCKS)]
+        prof = {}
 
-        for plane in (w2_plane_raw, tab_plane, lowered[0], lowered[1], w4_plane):
+        for plane in (tab_plane, w2_plane_raw, lowered[0], lowered[1], w4_plane):
             nc.vector.memset(plane[:].bitcast(I32), 0)
 
-        for q in range(4):
-            r0 = 32 * q + TAB_ROW
-            nc.gpsimd.dma_start(out=tab_plane[r0:r0 + 4 * PASSES, :].bitcast(I32),
-                                in_=tab_scales[:, 4 * q:4 * q + 4, :].bitcast(I32))
-
         weights = {0: w1, 2: w3}
-        raw, quant, total, hq = {}, {}, {}, {}
+        raw, quant, total, bent, hq = {}, {}, {}, {}, {}
 
         def load_table(a):
             nc.sync.dma_start(out=table[a][:], in_=tab_words[a].rearrange("p n i -> p (n i)").bitcast(I32))
 
-        def load_chunk(key):
+        def load_chunk(key, parts=1):
             b, a, i = key
-            raw[key] = ring.tile([P, PACK, KP], F32, name="raw", bufs=6)
-            rows = weights[i][a * KP:(a + 1) * KP, b * KP:(b + 1) * KP]
-            nc.sync.dma_start(out=raw[key][:], in_=rows.rearrange("(p j) c -> p j c", j=PACK))
+            width = KP // parts
+            raw[key] = []
+            for c0 in range(b * KP, (b + 1) * KP, width):
+                part = ring.tile([P, PACK, width], F32, name="stream", bufs=STREAM_BUFS, align_bytes=64)
+                rows = weights[i][a * KP:(a + 1) * KP, c0:c0 + width]
+                nc.sync.dma_start(out=part[:], in_=rows.rearrange("(p j) c -> p j c", j=PACK))
+                raw[key].append(part[:])
 
         def load_profile(b):
+            prof[b] = ring.tile([P, PACK, S], F32, name="stream", bufs=STREAM_BUFS, align_bytes=64)
             nc.sync.dma_start(out=prof[b][:],
                               in_=profile[b * KP:(b + 1) * KP, :].rearrange("(p t) s -> p t s", t=PACK))
 
@@ -82,17 +84,23 @@ def tile_list_preposition_slot_scores_kernel(
             for i in range(3):
                 nc.vector.tensor_copy(picked[i][a][:], table[a][:].bitcast(U32).indirect(lists[i][:]))
 
-        def quantize_chunk(key, on_vector):
+        def quantize_chunk(key, vector_halves, parts=1):
             grouped = ring.tile([P, PACK * P * PACK], BF16, name="grouped", bufs=3, align_bytes=64)
             dst = grouped[:].rearrange("p (t m j) -> p m j t", t=PACK, j=PACK)
-            src = raw[key][:].rearrange("p j (m t) -> p m j t", t=PACK)
-            if on_vector:
-                nc.vector.tensor_copy(out=dst, in_=src)
-            else:
-                nc.scalar.copy(out=dst, in_=src)
-            codes = ring.tile([P, KP], U32, name="codes", bufs=8, align_bytes=64)
-            plane = ring.tile([P, KP], U8, name="plane", bufs=8, align_bytes=64)
-            nc.vector.quantize_mx(out=codes[:].bitcast(FP8X4), scales=plane[:], in_=grouped[:])
+            for half in range(len(raw[key])):
+                src = raw[key][half].rearrange("p j (m t) -> p m j t", t=PACK)
+                rows = P // len(raw[key])
+                part = dst[:, half * rows:(half + 1) * rows]
+                if half in vector_halves:
+                    nc.vector.tensor_copy(out=part, in_=src)
+                else:
+                    nc.scalar.copy(out=part, in_=src)
+            codes = ring.tile([P, KP], U32, name="codes", bufs=6, align_bytes=64)
+            plane = ring.tile([P, KP], U8, name="plane", bufs=6, align_bytes=64)
+            width = KP // parts
+            for c0 in range(0, KP, width):
+                nc.vector.quantize_mx(out=codes[:, c0:c0 + width].bitcast(FP8X4), scales=plane[:, c0:c0 + width],
+                                      in_=grouped[:, PACK * c0:PACK * (c0 + width)])
             quant[key] = (codes, plane)
 
         def multiply(key, first, last):
@@ -114,21 +122,24 @@ def tile_list_preposition_slot_scores_kernel(
                                     rhs=picked[i][a][:].bitcast(FP8X4), rhs_scale=rhs_scale,
                                     start=first, stop=last)
 
-        def epilogue(b, s0, width):
+        def bend(b):
+            bent[b] = ring.tile([P, PACK, S], F32, name="bent", bufs=2)
+            for t in range(PACK):
+                nc.scalar.activation(out=bent[b][:, t, :], in_=total[b][t][:], func=ACT.Tanh,
+                                     bias=bias_sb[:, b, t:t + 1])
+                nc.vector.scalar_tensor_tensor(out=bent[b][:, t, :], in0=bent[b][:, t, :],
+                                               scalar=gain_sb[:, b, t:t + 1], in1=prof[b][:, t, :],
+                                               op0=ALU.mult, op1=ALU.mult)
+
+        def join(b, s0, width):
             cols = slice(s0, s0 + width)
-            bent = ring.tile([P, PACK, width], F32, name="bent", bufs=2)
             straight = ring.tile([P, PACK, width], F32, name="straight", bufs=2)
             for t in range(PACK):
-                nc.scalar.activation(out=bent[:, t, :], in_=total[b][t][:, cols], func=ACT.Tanh,
-                                     bias=bias_sb[:, b, t:t + 1])
                 nc.scalar.activation(out=straight[:, t, :], in_=total[b][t][:, cols], func=ACT.Identity,
                                      bias=gain_bias[:, b, t:t + 1], scale=gain_sb[:, b, t:t + 1])
-            for t in range(PACK):
-                nc.vector.scalar_tensor_tensor(out=bent[:, t, :], in0=bent[:, t, :], scalar=gain_sb[:, b, t:t + 1],
-                                               in1=prof[b][:, t, cols], op0=ALU.mult, op1=ALU.mult)
             h = ring.tile([P, width * PACK], BF16, name="h", bufs=2, align_bytes=64)
             nc.vector.tensor_tensor(out=h[:].rearrange("p (c i t) -> p c t i", i=4, t=PACK),
-                                    in0=bent[:].rearrange("p t (c i) -> p c t i", i=4),
+                                    in0=bent[b][:, :, cols].rearrange("p t (c i) -> p c t i", i=4),
                                     in1=straight[:].rearrange("p t (c i) -> p c t i", i=4), op=ALU.add)
             codes = held.tile([P, width], U32, name="hc%d_%d" % (b, s0), align_bytes=64)
             plane = held.tile([P, width], U8, name="hp%d_%d" % (b, s0), align_bytes=64)
@@ -168,89 +179,77 @@ def tile_list_preposition_slot_scores_kernel(
         nc.sync.dma_start(out=w2_raw[:].bitcast(I32).rearrange("p (a c) -> p a c", a=PASSES),
                           in_=w2_words.bitcast(I32).rearrange("a p c -> p a c"))
         for q in range(4):
+            r0 = 32 * q + TAB_ROW
+            nc.sync.dma_start(out=tab_plane[r0:r0 + 4 * PASSES, :].bitcast(I32),
+                              in_=tab_scales[:, 4 * q:4 * q + 4, :].bitcast(I32))
+        nc.sync.dma_start(lists[1][:], offs2)
+        nc.sync.dma_start(lists[0][:], offs)
+        load_chunk(chunks[0])
+        load_table(0)
+        nc.sync.dma_start(lists[2][:], offs3)
+        for q in range(4):
             nc.sync.dma_start(
                 out=w2_plane_raw[32 * q:32 * q + 4, :].bitcast(I32).rearrange("r (a c) -> r a c", a=PASSES),
                 in_=w2_scales[:, 4 * q:4 * q + 4, :].bitcast(I32).rearrange("a r c -> r a c"))
-        load_chunk(chunks[0])
-        load_table(0)
-        for tile, src in zip(lists, (offs, offs2, offs3)):
-            nc.sync.dma_start(tile[:], src)
         load_chunk(chunks[1])
-        load_chunk(chunks[2])
-        load_table(1)
-        for key in chunks[3:5]:
-            load_chunk(key)
-        nc.sync.dma_start(out=bias_sb[:], in_=bias.rearrange("(b p t) -> p b t", p=P, t=PACK))
-        nc.sync.dma_start(out=gain_sb[:], in_=gain.rearrange("(b p t) -> p b t", p=P, t=PACK))
 
         nc.vector.tensor_copy(out=w2_codes[:].bitcast(U16).rearrange("p (g t m) -> p g t m", t=PACK, m=P),
                               in_=w2_raw[:].bitcast(U16).rearrange("p (g m t) -> p g t m", t=PACK, m=P))
-        nc.vector.tensor_copy(out=w2_plane[:].rearrange("p (g t m) -> p g t m", t=PACK, m=P),
-                              in_=w2_plane_raw[:].rearrange("p (g m t) -> p g t m", t=PACK, m=P))
-        quantize_chunk(chunks[0], False)
-        for i in (1, 0, 2):
-            nc.vector.tensor_copy(picked_plane[i][:], tab_plane[:].indirect(lists[i][:]))
+        nc.vector.tensor_copy(picked_plane[1][:], tab_plane[:].indirect(lists[1][:]))
         for a in range(PASSES):
             r0 = TAB_ROW + 4 * a
-            nc.gpsimd.dma_start(out=lowered[a][0:P - 16, :].bitcast(I32),
-                                in_=picked_plane[1][r0:r0 + P - 16, :].bitcast(I32))
-        gather_words(0)
-        quantize_chunk(chunks[1], False)
-        quantize_chunk(chunks[2], False)
-        nc.vector.tensor_tensor(out=gain_bias[:], in0=gain_sb[:], in1=bias_sb[:], op=ALU.mult)
-        load_chunk(chunks[5])
-        load_chunk(chunks[6])
-        load_chunk(chunks[7])
-        load_profile(0)
-        multiply(chunks[0], True, False)
-        multiply(chunks[1], False, False)
-        gather_words(1)
-        quantize_chunk(chunks[3], False)
-        multiply((0, 0, 1), False, False)
-        multiply(chunks[2], False, False)
-        multiply((0, 1, 1), False, False)
-        multiply(chunks[3], False, True)
-
-        multiply((1, 0, 1), True, False)
-        multiply((1, 1, 1), False, False)
-        quantize_chunk(chunks[4], False)
-        load_chunk(chunks[8])
-        for q in range(4):
-            r0 = 32 * q + W4_ROW
-            nc.sync.dma_start(
-                out=w4_plane[r0:r0 + 4, :].bitcast(I32).rearrange("r (a c) -> r a c", a=BLOCKS),
-                in_=w4_scales[:, 4 * q:4 * q + 4, :].bitcast(I32).rearrange("a r c -> r a c"))
-        load_chunk(chunks[9])
-        load_profile(1)
-        multiply(chunks[4], False, False)
-        quantize_chunk(chunks[5], True)
-        load_chunk(chunks[10])
-        multiply(chunks[5], False, False)
-        quantize_chunk(chunks[6], True)
-        load_chunk(chunks[11])
+            nc.sync.dma_start(out=lowered[a][0:P - 16, :].bitcast(I32),
+                              in_=picked_plane[1][r0:r0 + P - 16, :].bitcast(I32))
+        load_table(1)
+        nc.sync.dma_start(out=bias_sb[:], in_=bias.rearrange("(b p t) -> p b t", p=P, t=PACK))
+        nc.sync.dma_start(out=gain_sb[:], in_=gain.rearrange("(b p t) -> p b t", p=P, t=PACK))
+        last = len(chunks) - 1
+        for n in range(2, last + 1):
+            load_chunk(chunks[n], 2 if n == last else 1)
+            if n == PROFILE_AFTER[0]:
+                load_profile(0)
+            if n == PROFILE_AFTER[1]:
+                load_profile(1)
+            if n == 8:
+                for q in range(4):
+                    r0 = 32 * q + W4_ROW
+                    nc.sync.dma_start(
+                        out=w4_plane[r0:r0 + 4, :].bitcast(I32).rearrange("r (a c) -> r a c", a=BLOCKS),
+                        in_=w4_scales[:, 4 * q:4 * q + 4, :].bitcast(I32).rearrange("a r c -> r a c"))
+        load_profile(2)
+        w4_codes = ring.tile([P, BLOCKS * N], I32, name="stream", bufs=STREAM_BUFS, align_bytes=64)
         nc.sync.dma_start(out=w4_codes[:].rearrange("p (a c) -> p a c", a=BLOCKS),
                           in_=w4_words.rearrange("a p c i -> p a (c i)").bitcast(I32))
-        load_profile(2)
-        multiply(chunks[6], False, False)
-        quantize_chunk(chunks[7], False)
-        epilogue(0, 0, S)
-        multiply(chunks[7], False, True)
 
-        multiply((2, 0, 1), True, False)
-        multiply((2, 1, 1), False, False)
-        quantize_chunk(chunks[8], False)
-        multiply(chunks[8], False, False)
-        epilogue(1, 0, S)
-        quantize_chunk(chunks[9], True)
-        multiply(chunks[9], False, False)
-        quantize_chunk(chunks[10], False)
-        multiply(chunks[10], False, False)
-        quantize_chunk(chunks[11], True)
-        multiply(chunks[11], False, True)
+        nc.vector.tensor_copy(picked_plane[0][:], tab_plane[:].indirect(lists[0][:]))
+        quantize_chunk(chunks[0], ())
+        nc.vector.tensor_copy(picked_plane[2][:], tab_plane[:].indirect(lists[2][:]))
+        gather_words(0)
+        quantize_chunk(chunks[1], ())
+        nc.vector.tensor_copy(out=w2_plane[:].rearrange("p (g t m) -> p g t m", t=PACK, m=P),
+                              in_=w2_plane_raw[:].rearrange("p (g m t) -> p g t m", t=PACK, m=P))
+        gather_words(1)
+        nc.vector.tensor_tensor(out=gain_bias[:], in0=gain_sb[:], in1=bias_sb[:], op=ALU.mult)
+
+        for b in range(BLOCKS):
+            keys = [(b, a, i) for a in range(PASSES) for i in (1, 0, 2)]
+            for key in keys:
+                if key in chunks and key not in quant:
+                    n = chunks.index(key)
+                    if n == last:
+                        quantize_chunk(key, (1,), PACK)
+                    else:
+                        quantize_chunk(key, (0,) if n in ON_VECTOR else ())
+                multiply(key, key == keys[0], key == keys[-1])
+            if b < BLOCKS - 1:
+                bend(b)
+                join(b, 0, S)
         for b in range(BLOCKS - 1):
             for half in range(2):
                 score(b, half)
+        bend(BLOCKS - 1)
         for half in range(2):
-            epilogue(2, half * HALF, HALF)
-            score(2, half)
+            join(BLOCKS - 1, half * HALF, HALF)
+        for half in range(2):
+            score(BLOCKS - 1, half)
             store(half)

@@ -22,11 +22,11 @@ KP = P * PACK
 PASSES = K // KP
 BLOCKS = H // KP
 HALF = S // 2
-TAB_ROW = 4
+LIFT = 16
 W4_ROW = 12
-PROFILE_AFTER = (4, 10)
-STREAM_BUFS = 4
-ON_VECTOR = (5, 9, 10)
+PROFILE_AFTER = (5, 9)
+STREAM_BUFS = 10
+ON_VECTOR = (4, 5, 9)
 
 
 def tile_list_preposition_slot_scores_kernel(
@@ -44,19 +44,19 @@ def tile_list_preposition_slot_scores_kernel(
         tab_plane = held.tile([P, T], U8, align_bytes=64)
         picked = [[held.tile([P, S], U32, name="picked%d_%d" % (i, a), align_bytes=64) for a in range(PASSES)]
                   for i in range(3)]
-        picked_plane = [held.tile([P, S], U8, name="pplane%d" % i, align_bytes=64) for i in range(3)]
-        lowered = [held.tile([P, S], U8, name="lowered%d" % a, align_bytes=64) for a in range(PASSES)]
+        picked_plane = held.tile([P, 3 * S], U8, align_bytes=64)
+        lowered = held.tile([P, 3 * S], U8, align_bytes=64)
         w2_raw = held.tile([P, PASSES * 2 * H], U8, align_bytes=64)
         w2_codes = held.tile([P, PASSES * 2 * H], U8, align_bytes=64)
         w2_plane_raw = held.tile([P, PASSES * H], U8, align_bytes=64)
         w2_plane = held.tile([P, PASSES * H], U8, align_bytes=64)
         w4_plane = held.tile([P, BLOCKS * N], U8, align_bytes=64)
-        bias_sb = held.tile([P, BLOCKS, PACK], F32)
-        gain_sb = held.tile([P, BLOCKS, PACK], F32)
+        bias_sb = held.tile([P, BLOCKS, 2 * PACK], F32)
+        gain_sb = held.tile([P, BLOCKS, 2 * PACK], F32)
         gain_bias = held.tile([P, BLOCKS, PACK], F32)
         prof = {}
 
-        for plane in (tab_plane, w2_plane_raw, lowered[0], lowered[1], w4_plane):
+        for plane in (tab_plane, w2_plane_raw, lowered, w4_plane):
             nc.vector.memset(plane[:].bitcast(I32), 0)
 
         weights = {0: w1, 2: w3}
@@ -107,17 +107,16 @@ def tile_list_preposition_slot_scores_kernel(
             b, a, i = key
             if first:
                 total[b] = [psum.tile([P, S], F32, name="bank%d" % (4 * (b % 2) + t)) for t in range(PACK)]
+            rhs_scale = (picked_plane, lowered)[a][:, i * S:(i + 1) * S]
             for t in range(PACK):
                 if i == 1:
                     c0 = a * H + b * KP + t * P
                     lhs = w2_codes[:, 2 * c0:2 * (c0 + P)].bitcast(FP4X4)
                     lhs_scale = w2_plane[:, c0:c0 + P]
-                    rhs_scale = lowered[a][:]
                 else:
                     codes, plane = quant[key]
                     lhs = codes[:, t * P:(t + 1) * P].bitcast(FP8X4)
                     lhs_scale = plane[:, t * P:(t + 1) * P]
-                    rhs_scale = picked_plane[i][TAB_ROW + 4 * a:P, :]
                 nc.tensor.matmul_mx(out=total[b][t][:], lhsT=lhs, lhsT_scale=lhs_scale,
                                     rhs=picked[i][a][:].bitcast(FP8X4), rhs_scale=rhs_scale,
                                     start=first, stop=last)
@@ -178,15 +177,14 @@ def tile_list_preposition_slot_scores_kernel(
 
         nc.sync.dma_start(out=w2_raw[:].bitcast(I32).rearrange("p (a c) -> p a c", a=PASSES),
                           in_=w2_words.bitcast(I32).rearrange("a p c -> p a c"))
-        for q in range(4):
-            r0 = 32 * q + TAB_ROW
-            nc.sync.dma_start(out=tab_plane[r0:r0 + 4 * PASSES, :].bitcast(I32),
-                              in_=tab_scales[:, 4 * q:4 * q + 4, :].bitcast(I32))
-        nc.sync.dma_start(lists[1][:], offs2)
+        for r in range(4):
+            nc.sync.dma_start(out=tab_plane[r:P:LIFT, :].bitcast(I32),
+                              in_=tab_scales[:, r:16:4, :].bitcast(I32).rearrange("a q c -> q a c"))
         nc.sync.dma_start(lists[0][:], offs)
+        nc.sync.dma_start(lists[1][:], offs2)
         load_chunk(chunks[0])
-        load_table(0)
         nc.sync.dma_start(lists[2][:], offs3)
+        load_table(0)
         for q in range(4):
             nc.sync.dma_start(
                 out=w2_plane_raw[32 * q:32 * q + 4, :].bitcast(I32).rearrange("r (a c) -> r a c", a=PASSES),
@@ -195,16 +193,15 @@ def tile_list_preposition_slot_scores_kernel(
 
         nc.vector.tensor_copy(out=w2_codes[:].bitcast(U16).rearrange("p (g t m) -> p g t m", t=PACK, m=P),
                               in_=w2_raw[:].bitcast(U16).rearrange("p (g m t) -> p g t m", t=PACK, m=P))
-        nc.vector.tensor_copy(picked_plane[1][:], tab_plane[:].indirect(lists[1][:]))
-        for a in range(PASSES):
-            r0 = TAB_ROW + 4 * a
-            nc.sync.dma_start(out=lowered[a][0:P - 16, :].bitcast(I32),
-                              in_=picked_plane[1][r0:r0 + P - 16, :].bitcast(I32))
+        for i in range(3):
+            nc.vector.tensor_copy(picked_plane[:, i * S:(i + 1) * S], tab_plane[:].indirect(lists[i][:]))
+        nc.sync.dma_start(out=lowered[0:P - LIFT, :].bitcast(I32), in_=picked_plane[LIFT:P, :].bitcast(I32))
+        load_chunk(chunks[2])
         load_table(1)
-        nc.sync.dma_start(out=bias_sb[:], in_=bias.rearrange("(b p t) -> p b t", p=P, t=PACK))
-        nc.sync.dma_start(out=gain_sb[:], in_=gain.rearrange("(b p t) -> p b t", p=P, t=PACK))
+        nc.sync.dma_start(out=bias_sb[:, :, 0:PACK], in_=bias.rearrange("(b p t) -> p b t", p=P, t=PACK))
+        nc.sync.dma_start(out=gain_sb[:, :, 0:PACK], in_=gain.rearrange("(b p t) -> p b t", p=P, t=PACK))
         last = len(chunks) - 1
-        for n in range(2, last + 1):
+        for n in range(3, last + 1):
             load_chunk(chunks[n], 2 if n == last else 1)
             if n == PROFILE_AFTER[0]:
                 load_profile(0)
@@ -221,15 +218,13 @@ def tile_list_preposition_slot_scores_kernel(
         nc.sync.dma_start(out=w4_codes[:].rearrange("p (a c) -> p a c", a=BLOCKS),
                           in_=w4_words.rearrange("a p c i -> p a (c i)").bitcast(I32))
 
-        nc.vector.tensor_copy(picked_plane[0][:], tab_plane[:].indirect(lists[0][:]))
         quantize_chunk(chunks[0], ())
-        nc.vector.tensor_copy(picked_plane[2][:], tab_plane[:].indirect(lists[2][:]))
         gather_words(0)
         quantize_chunk(chunks[1], ())
         nc.vector.tensor_copy(out=w2_plane[:].rearrange("p (g t m) -> p g t m", t=PACK, m=P),
                               in_=w2_plane_raw[:].rearrange("p (g m t) -> p g t m", t=PACK, m=P))
         gather_words(1)
-        nc.vector.tensor_tensor(out=gain_bias[:], in0=gain_sb[:], in1=bias_sb[:], op=ALU.mult)
+        nc.vector.tensor_tensor(out=gain_bias[:], in0=gain_sb[:, :, 0:PACK], in1=bias_sb[:, :, 0:PACK], op=ALU.mult)
 
         for b in range(BLOCKS):
             keys = [(b, a, i) for a in range(PASSES) for i in (1, 0, 2)]

@@ -20,13 +20,21 @@ P = 128
 PACK = 4
 KP = P * PACK
 PASSES = K // KP
-BLOCKS = H // KP
-HALF = S // 2
+BANDS = H // KP
+LOOKUPS = 3
+QUADRANT = 32
+QUADRANTS = P // QUADRANT
+SCALE_ROWS = 4
 LIFT = 16
 W4_ROW = 12
-PROFILE_AFTER = (5, 9)
-STREAM_BUFS = 10
-ON_VECTOR = (4, 5, 9)
+PIECES = 4
+PIECE = S // PIECES
+RUN = 4
+STREAM_BUFS = 8
+GROUPED_BUFS = 3
+CODE_BUFS = 6
+BENT_BUFS = 2
+JOIN_BUFS = 3
 
 
 def tile_list_preposition_slot_scores_kernel(
@@ -39,35 +47,43 @@ def tile_list_preposition_slot_scores_kernel(
         ring = ctx.enter_context(tc.tile_pool(name="ring", bufs=1))
         psum = ctx.enter_context(tc.psum_pool(name="psum", bufs=1))
 
-        lists = [held.tile([P, S // 16], U16, name="list%d" % i) for i in range(3)]
+        lists = [held.tile([P, S // 16], U16, name="list%d" % i) for i in range(LOOKUPS)]
         table = [held.tile([P, T], I32, name="table%d" % a, align_bytes=64) for a in range(PASSES)]
         tab_plane = held.tile([P, T], U8, align_bytes=64)
         picked = [[held.tile([P, S], U32, name="picked%d_%d" % (i, a), align_bytes=64) for a in range(PASSES)]
-                  for i in range(3)]
-        picked_plane = held.tile([P, 3 * S], U8, align_bytes=64)
-        lowered = held.tile([P, 3 * S], U8, align_bytes=64)
+                  for i in range(LOOKUPS)]
+        picked_plane = held.tile([P, LOOKUPS * S], U8, align_bytes=64)
+        lowered_plane = held.tile([P, LOOKUPS * S], U8, align_bytes=64)
         w2_raw = held.tile([P, PASSES * 2 * H], U8, align_bytes=64)
         w2_codes = held.tile([P, PASSES * 2 * H], U8, align_bytes=64)
         w2_plane_raw = held.tile([P, PASSES * H], U8, align_bytes=64)
         w2_plane = held.tile([P, PASSES * H], U8, align_bytes=64)
-        w4_plane = held.tile([P, BLOCKS * N], U8, align_bytes=64)
-        bias_sb = held.tile([P, BLOCKS, 2 * PACK], F32)
-        gain_sb = held.tile([P, BLOCKS, 2 * PACK], F32)
-        gain_bias = held.tile([P, BLOCKS, PACK], F32)
-        prof = {}
+        w4_plane = held.tile([P, BANDS * N], U8, align_bytes=64)
+        bias_sb = held.tile([P, BANDS, 2 * PACK], F32)
+        gain_sb = held.tile([P, BANDS, 2 * PACK], F32)
+        gain_bias = held.tile([P, BANDS, PACK], F32)
 
-        for plane in (tab_plane, w2_plane_raw, lowered, w4_plane):
+        for plane in (tab_plane, w2_plane_raw, lowered_plane, w4_plane):
             nc.vector.memset(plane[:].bitcast(I32), 0)
 
         weights = {0: w1, 2: w3}
-        raw, quant, total, bent, hq = {}, {}, {}, {}, {}
+        raw, quantised, total, prof, bent, h_mx, scores = {}, {}, {}, {}, {}, {}, {}
+        chunks = [(b, a, i) for b in range(BANDS) for a in range(PASSES) for i in weights]
+        last_chunk = chunks[-1]
 
         def load_table(a):
             nc.sync.dma_start(out=table[a][:], in_=tab_words[a].rearrange("p n i -> p (n i)").bitcast(I32))
 
-        def load_chunk(key, parts=1):
+        def load_planes(plane, row, scales):
+            for q in range(QUADRANTS):
+                r0 = QUADRANT * q + row
+                nc.sync.dma_start(
+                    out=plane[r0:r0 + SCALE_ROWS, :].bitcast(I32).rearrange("r (a c) -> r a c", a=scales.shape[0]),
+                    in_=scales[:, SCALE_ROWS * q:SCALE_ROWS * (q + 1), :].bitcast(I32).rearrange("a r c -> r a c"))
+
+        def load_chunk(key):
             b, a, i = key
-            width = KP // parts
+            width = KP // 2 if key == last_chunk else KP
             raw[key] = []
             for c0 in range(b * KP, (b + 1) * KP, width):
                 part = ring.tile([P, PACK, width], F32, name="stream", bufs=STREAM_BUFS, align_bytes=64)
@@ -81,48 +97,49 @@ def tile_list_preposition_slot_scores_kernel(
                               in_=profile[b * KP:(b + 1) * KP, :].rearrange("(p t) s -> p t s", t=PACK))
 
         def gather_words(a):
-            for i in range(3):
+            for i in range(LOOKUPS):
                 nc.vector.tensor_copy(picked[i][a][:], table[a][:].bitcast(U32).indirect(lists[i][:]))
 
-        def quantize_chunk(key, vector_halves, parts=1):
-            grouped = ring.tile([P, PACK * P * PACK], BF16, name="grouped", bufs=3, align_bytes=64)
-            dst = grouped[:].rearrange("p (t m j) -> p m j t", t=PACK, j=PACK)
-            for half in range(len(raw[key])):
-                src = raw[key][half].rearrange("p j (m t) -> p m j t", t=PACK)
-                rows = P // len(raw[key])
-                part = dst[:, half * rows:(half + 1) * rows]
-                if half in vector_halves:
-                    nc.vector.tensor_copy(out=part, in_=src)
+        def quantize_chunk(key):
+            b, a, i = key
+            grouped = ring.tile([P, PACK * P * PACK], BF16, name="grouped", bufs=GROUPED_BUFS, align_bytes=64)
+            dealt = grouped[:].rearrange("p (t m j) -> p m j t", t=PACK, j=PACK)
+            span = P // len(raw[key])
+            for n, part in enumerate(raw[key]):
+                src = part.rearrange("p j (m t) -> p m j t", t=PACK)
+                dst = dealt[:, n * span:(n + 1) * span]
+                if (b > 0 and a == 0) or n == 1:
+                    nc.vector.tensor_copy(out=dst, in_=src)
                 else:
-                    nc.scalar.copy(out=part, in_=src)
-            codes = ring.tile([P, KP], U32, name="codes", bufs=6, align_bytes=64)
-            plane = ring.tile([P, KP], U8, name="plane", bufs=6, align_bytes=64)
-            width = KP // parts
+                    nc.scalar.copy(out=dst, in_=src)
+            codes = ring.tile([P, KP], U32, name="codes", bufs=CODE_BUFS, align_bytes=64)
+            plane = ring.tile([P, KP], U8, name="plane", bufs=CODE_BUFS, align_bytes=64)
+            width = P if key == last_chunk else KP
             for c0 in range(0, KP, width):
                 nc.vector.quantize_mx(out=codes[:, c0:c0 + width].bitcast(FP8X4), scales=plane[:, c0:c0 + width],
                                       in_=grouped[:, PACK * c0:PACK * (c0 + width)])
-            quant[key] = (codes, plane)
+            quantised[key] = (codes, plane)
 
         def multiply(key, first, last):
             b, a, i = key
             if first:
-                total[b] = [psum.tile([P, S], F32, name="bank%d" % (4 * (b % 2) + t)) for t in range(PACK)]
-            rhs_scale = (picked_plane, lowered)[a][:, i * S:(i + 1) * S]
+                total[b] = [psum.tile([P, S], F32, name="bank%d" % (PACK * (b % 2) + t)) for t in range(PACK)]
+            rhs_scale = (picked_plane, lowered_plane)[a][:, i * S:(i + 1) * S]
             for t in range(PACK):
-                if i == 1:
+                if i in weights:
+                    codes, plane = quantised[key]
+                    lhs = codes[:, t * P:(t + 1) * P].bitcast(FP8X4)
+                    lhs_scale = plane[:, t * P:(t + 1) * P]
+                else:
                     c0 = a * H + b * KP + t * P
                     lhs = w2_codes[:, 2 * c0:2 * (c0 + P)].bitcast(FP4X4)
                     lhs_scale = w2_plane[:, c0:c0 + P]
-                else:
-                    codes, plane = quant[key]
-                    lhs = codes[:, t * P:(t + 1) * P].bitcast(FP8X4)
-                    lhs_scale = plane[:, t * P:(t + 1) * P]
                 nc.tensor.matmul_mx(out=total[b][t][:], lhsT=lhs, lhsT_scale=lhs_scale,
                                     rhs=picked[i][a][:].bitcast(FP8X4), rhs_scale=rhs_scale,
                                     start=first, stop=last)
 
         def bend(b):
-            bent[b] = ring.tile([P, PACK, S], F32, name="bent", bufs=2)
+            bent[b] = ring.tile([P, PACK, S], F32, name="bent", bufs=BENT_BUFS)
             for t in range(PACK):
                 nc.scalar.activation(out=bent[b][:, t, :], in_=total[b][t][:], func=ACT.Tanh,
                                      bias=bias_sb[:, b, t:t + 1])
@@ -132,119 +149,101 @@ def tile_list_preposition_slot_scores_kernel(
 
         def join(b, s0, width):
             cols = slice(s0, s0 + width)
-            straight = ring.tile([P, PACK, width], F32, name="straight", bufs=2)
+            straight = ring.tile([P, PACK, width], F32, name="straight", bufs=JOIN_BUFS)
             for t in range(PACK):
                 nc.scalar.activation(out=straight[:, t, :], in_=total[b][t][:, cols], func=ACT.Identity,
                                      bias=gain_bias[:, b, t:t + 1], scale=gain_sb[:, b, t:t + 1])
-            h = ring.tile([P, width * PACK], BF16, name="h", bufs=2, align_bytes=64)
-            nc.vector.tensor_tensor(out=h[:].rearrange("p (c i t) -> p c t i", i=4, t=PACK),
-                                    in0=bent[b][:, :, cols].rearrange("p t (c i) -> p c t i", i=4),
-                                    in1=straight[:].rearrange("p t (c i) -> p c t i", i=4), op=ALU.add)
-            codes = held.tile([P, width], U32, name="hc%d_%d" % (b, s0), align_bytes=64)
-            plane = held.tile([P, width], U8, name="hp%d_%d" % (b, s0), align_bytes=64)
+            h = ring.tile([P, width * PACK], BF16, name="h", bufs=JOIN_BUFS, align_bytes=64)
+            nc.vector.tensor_tensor(out=h[:].rearrange("p (c e t) -> p c t e", e=RUN, t=PACK),
+                                    in0=bent[b][:, :, cols].rearrange("p t (c e) -> p c t e", e=RUN),
+                                    in1=straight[:].rearrange("p t (c e) -> p c t e", e=RUN), op=ALU.add)
+            codes = held.tile([P, width], U32, name="h_codes%d_%d" % (b, s0), align_bytes=64)
+            plane = held.tile([P, width], U8, name="h_plane%d_%d" % (b, s0), align_bytes=64)
             nc.vector.quantize_mx(out=codes[:].bitcast(FP8X4), scales=plane[:], in_=h[:])
-            for half in range(s0 // HALF, (s0 + width) // HALF):
-                c = slice(half * HALF - s0, (half + 1) * HALF - s0)
-                hq[(b, half)] = (codes[:, c], plane[:, c])
+            for c0 in range(0, width, PIECE):
+                h_mx[(b, (s0 + c0) // PIECE)] = (codes[:, c0:c0 + PIECE], plane[:, c0:c0 + PIECE])
 
-        scores = {}
-
-        def score(b, half):
+        def score(b, piece):
             if b == 0:
-                for pair in range(2):
-                    scores[(half, pair)] = psum.tile([P, 2, HALF], F32, name="bank%d" % (4 + 2 * half + pair))
-            codes, plane = hq[(b, half)]
+                scores[piece] = psum.tile([P, N // P, PIECE], F32, name="bank%d" % (PACK + piece))
+            codes, plane = h_mx[(b, piece)]
             for m in range(N // P):
                 c0 = b * N + m * P
-                nc.tensor.matmul_mx(out=scores[(half, m // 2)][:, m % 2, :],
+                nc.tensor.matmul_mx(out=scores[piece][:, m, :],
                                     lhsT=w4_codes[:, c0:c0 + P].bitcast(FP8X4),
                                     lhsT_scale=w4_plane[W4_ROW:P, c0:c0 + P],
                                     rhs=codes.bitcast(FP8X4), rhs_scale=plane,
-                                    start=(b == 0 and m % 2 == 0), stop=(b == BLOCKS - 1 and m % 2 == 1))
+                                    start=(b == 0 and m == 0), stop=(b == BANDS - 1 and m == N // P - 1))
 
-        def store(half):
-            for pair in range(2):
-                staged = held.tile([P, 2, HALF], F32, name="staged%d_%d" % (half, pair))
-                dst = out[2 * pair * P:2 * (pair + 1) * P, half * HALF:(half + 1) * HALF]
-                dst = dst.rearrange("(m p) s -> p m s", p=P)
-                if pair == 0:
-                    nc.scalar.copy(out=staged[:], in_=scores[(half, pair)][:])
-                else:
-                    nc.vector.tensor_copy(out=staged[:], in_=scores[(half, pair)][:])
-                nc.sync.dma_start(out=dst, in_=staged[:])
-
-        chunks = [(b, a, i) for b in range(BLOCKS) for a in range(PASSES) for i in (0, 2)]
+        def store(piece):
+            staged = held.tile([P, N // P, PIECE], F32, name="staged%d" % piece)
+            if piece == PIECES - 1:
+                nc.vector.tensor_copy(out=staged[:], in_=scores[piece][:])
+            else:
+                nc.scalar.copy(out=staged[:], in_=scores[piece][:])
+            dst = out[:, piece * PIECE:(piece + 1) * PIECE].rearrange("(m p) s -> p m s", p=P)
+            nc.sync.dma_start(out=dst, in_=staged[:])
 
         nc.sync.dma_start(out=w2_raw[:].bitcast(I32).rearrange("p (a c) -> p a c", a=PASSES),
                           in_=w2_words.bitcast(I32).rearrange("a p c -> p a c"))
-        for r in range(4):
+        for r in range(SCALE_ROWS):
             nc.sync.dma_start(out=tab_plane[r:P:LIFT, :].bitcast(I32),
-                              in_=tab_scales[:, r:16:4, :].bitcast(I32).rearrange("a q c -> q a c"))
+                              in_=tab_scales[:, r::SCALE_ROWS, :].bitcast(I32).rearrange("a q c -> q a c"))
         nc.sync.dma_start(lists[0][:], offs)
         nc.sync.dma_start(lists[1][:], offs2)
         load_chunk(chunks[0])
         nc.sync.dma_start(lists[2][:], offs3)
         load_table(0)
-        for q in range(4):
-            nc.sync.dma_start(
-                out=w2_plane_raw[32 * q:32 * q + 4, :].bitcast(I32).rearrange("r (a c) -> r a c", a=PASSES),
-                in_=w2_scales[:, 4 * q:4 * q + 4, :].bitcast(I32).rearrange("a r c -> r a c"))
+        load_planes(w2_plane_raw, 0, w2_scales)
         load_chunk(chunks[1])
 
         nc.vector.tensor_copy(out=w2_codes[:].bitcast(U16).rearrange("p (g t m) -> p g t m", t=PACK, m=P),
                               in_=w2_raw[:].bitcast(U16).rearrange("p (g m t) -> p g t m", t=PACK, m=P))
-        for i in range(3):
+        for i in range(LOOKUPS):
             nc.vector.tensor_copy(picked_plane[:, i * S:(i + 1) * S], tab_plane[:].indirect(lists[i][:]))
-        nc.sync.dma_start(out=lowered[0:P - LIFT, :].bitcast(I32), in_=picked_plane[LIFT:P, :].bitcast(I32))
+        for r in range(SCALE_ROWS):
+            nc.sync.dma_start(out=lowered_plane[r:P:QUADRANT, :].bitcast(I32),
+                              in_=picked_plane[LIFT + r:P:QUADRANT, :].bitcast(I32))
+
         load_chunk(chunks[2])
         load_table(1)
         nc.sync.dma_start(out=bias_sb[:, :, 0:PACK], in_=bias.rearrange("(b p t) -> p b t", p=P, t=PACK))
         nc.sync.dma_start(out=gain_sb[:, :, 0:PACK], in_=gain.rearrange("(b p t) -> p b t", p=P, t=PACK))
-        last = len(chunks) - 1
-        for n in range(3, last + 1):
-            load_chunk(chunks[n], 2 if n == last else 1)
-            if n == PROFILE_AFTER[0]:
-                load_profile(0)
-            if n == PROFILE_AFTER[1]:
-                load_profile(1)
-            if n == 8:
-                for q in range(4):
-                    r0 = 32 * q + W4_ROW
-                    nc.sync.dma_start(
-                        out=w4_plane[r0:r0 + 4, :].bitcast(I32).rearrange("r (a c) -> r a c", a=BLOCKS),
-                        in_=w4_scales[:, 4 * q:4 * q + 4, :].bitcast(I32).rearrange("a r c -> r a c"))
-        load_profile(2)
-        w4_codes = ring.tile([P, BLOCKS * N], I32, name="stream", bufs=STREAM_BUFS, align_bytes=64)
-        nc.sync.dma_start(out=w4_codes[:].rearrange("p (a c) -> p a c", a=BLOCKS),
+        for key in chunks[3:]:
+            b, a, i = key
+            load_chunk(key)
+            if b > 0 and (a, i) == (0, 2):
+                load_profile(b - 1)
+            if key == (BANDS - 1, 0, 0):
+                load_planes(w4_plane, W4_ROW, w4_scales)
+        load_profile(BANDS - 1)
+        w4_codes = ring.tile([P, BANDS * N], I32, name="stream", bufs=STREAM_BUFS, align_bytes=64)
+        nc.sync.dma_start(out=w4_codes[:].rearrange("p (a c) -> p a c", a=BANDS),
                           in_=w4_words.rearrange("a p c i -> p a (c i)").bitcast(I32))
 
-        quantize_chunk(chunks[0], ())
+        quantize_chunk(chunks[0])
         gather_words(0)
-        quantize_chunk(chunks[1], ())
+        quantize_chunk(chunks[1])
         nc.vector.tensor_copy(out=w2_plane[:].rearrange("p (g t m) -> p g t m", t=PACK, m=P),
                               in_=w2_plane_raw[:].rearrange("p (g m t) -> p g t m", t=PACK, m=P))
         gather_words(1)
         nc.vector.tensor_tensor(out=gain_bias[:], in0=gain_sb[:, :, 0:PACK], in1=bias_sb[:, :, 0:PACK], op=ALU.mult)
 
-        for b in range(BLOCKS):
+        for b in range(BANDS):
             keys = [(b, a, i) for a in range(PASSES) for i in (1, 0, 2)]
             for key in keys:
-                if key in chunks and key not in quant:
-                    n = chunks.index(key)
-                    if n == last:
-                        quantize_chunk(key, (1,), PACK)
-                    else:
-                        quantize_chunk(key, (0,) if n in ON_VECTOR else ())
+                if key in raw and key not in quantised:
+                    quantize_chunk(key)
                 multiply(key, key == keys[0], key == keys[-1])
-            if b < BLOCKS - 1:
+            if b < BANDS - 1:
                 bend(b)
                 join(b, 0, S)
-        for b in range(BLOCKS - 1):
-            for half in range(2):
-                score(b, half)
-        bend(BLOCKS - 1)
-        for half in range(2):
-            join(BLOCKS - 1, half * HALF, HALF)
-        for half in range(2):
-            score(BLOCKS - 1, half)
-            store(half)
+        for b in range(BANDS - 1):
+            for piece in range(PIECES):
+                score(b, piece)
+        bend(BANDS - 1)
+        for piece in range(PIECES):
+            join(BANDS - 1, piece * PIECE, PIECE)
+        for piece in range(PIECES):
+            score(BANDS - 1, piece)
+            store(piece)

from contextlib import ExitStack

import concourse.mybir as mybir

K, T, S, H, N = 1024, 4096, 512, 1536, 512
FLOPS = 2 * (3 * K * H * S + H * N * S)

F32 = mybir.dt.float32
BF16 = mybir.dt.bfloat16
I32 = mybir.dt.int32
U32 = mybir.dt.uint32
U16 = mybir.dt.uint16
U8 = mybir.dt.uint8
FP8X4 = mybir.dt.float8_e4m3fn_x4
FP4X4 = mybir.dt.float4_e2m1fn_x4
ACT = mybir.ActivationFunctionType
ALU = mybir.AluOpType

P = 128
PACK = 4
KP = P * PACK
PASSES = K // KP
BANDS = H // KP
LOOKUPS = 3
QUADRANT = 32
QUADRANTS = P // QUADRANT
SCALE_ROWS = 4
LIFT = 16
W4_ROW = 12
PIECES = 4
PIECE = S // PIECES
RUN = 4
STREAM_BUFS = 8
GROUPED_BUFS = 3
CODE_BUFS = 6
BENT_BUFS = 2
JOIN_BUFS = 3


def tile_list_preposition_slot_scores_kernel(
    tc, tab_words, tab_scales, offs, offs2, offs3, w1, w2_words, w2_scales, w3,
    bias, profile, gain, w4_words, w4_scales, out,
):
    nc = tc.nc
    with ExitStack() as ctx:
        held = ctx.enter_context(tc.tile_pool(name="held", bufs=1))
        ring = ctx.enter_context(tc.tile_pool(name="ring", bufs=1))
        psum = ctx.enter_context(tc.psum_pool(name="psum", bufs=1))

        lists = [held.tile([P, S // 16], U16, name="list%d" % i) for i in range(LOOKUPS)]
        table = [held.tile([P, T], I32, name="table%d" % a, align_bytes=64) for a in range(PASSES)]
        tab_plane = held.tile([P, T], U8, align_bytes=64)
        picked = [[held.tile([P, S], U32, name="picked%d_%d" % (i, a), align_bytes=64) for a in range(PASSES)]
                  for i in range(LOOKUPS)]
        picked_plane = held.tile([P, LOOKUPS * S], U8, align_bytes=64)
        lowered_plane = held.tile([P, LOOKUPS * S], U8, align_bytes=64)
        w2_raw = held.tile([P, PASSES * 2 * H], U8, align_bytes=64)
        w2_codes = held.tile([P, PASSES * 2 * H], U8, align_bytes=64)
        w2_plane_raw = held.tile([P, PASSES * H], U8, align_bytes=64)
        w2_plane = held.tile([P, PASSES * H], U8, align_bytes=64)
        w4_plane = held.tile([P, BANDS * N], U8, align_bytes=64)
        bias_sb = held.tile([P, BANDS, 2 * PACK], F32)
        gain_sb = held.tile([P, BANDS, 2 * PACK], F32)
        gain_bias = held.tile([P, BANDS, PACK], F32)

        for plane in (tab_plane, w2_plane_raw, lowered_plane, w4_plane):
            nc.vector.memset(plane[:].bitcast(I32), 0)

        weights = {0: w1, 2: w3}
        raw, quantised, total, prof, bent, h_mx, scores = {}, {}, {}, {}, {}, {}, {}
        chunks = [(b, a, i) for b in range(BANDS) for a in range(PASSES) for i in weights]
        last_chunk = chunks[-1]

        def load_table(a):
            nc.sync.dma_start(out=table[a][:], in_=tab_words[a].rearrange("p n i -> p (n i)").bitcast(I32))

        def load_planes(plane, row, scales):
            for q in range(QUADRANTS):
                r0 = QUADRANT * q + row
                nc.sync.dma_start(
                    out=plane[r0:r0 + SCALE_ROWS, :].bitcast(I32).rearrange("r (a c) -> r a c", a=scales.shape[0]),
                    in_=scales[:, SCALE_ROWS * q:SCALE_ROWS * (q + 1), :].bitcast(I32).rearrange("a r c -> r a c"))

        def load_chunk(key):
            b, a, i = key
            width = KP // 2 if key == last_chunk else KP
            raw[key] = []
            for c0 in range(b * KP, (b + 1) * KP, width):
                part = ring.tile([P, PACK, width], F32, name="stream", bufs=STREAM_BUFS, align_bytes=64)
                rows = weights[i][a * KP:(a + 1) * KP, c0:c0 + width]
                nc.sync.dma_start(out=part[:], in_=rows.rearrange("(p j) c -> p j c", j=PACK))
                raw[key].append(part[:])

        def load_profile(b):
            prof[b] = ring.tile([P, PACK, S], F32, name="stream", bufs=STREAM_BUFS, align_bytes=64)
            nc.sync.dma_start(out=prof[b][:],
                              in_=profile[b * KP:(b + 1) * KP, :].rearrange("(p t) s -> p t s", t=PACK))

        def gather_words(a):
            for i in range(LOOKUPS):
                nc.vector.tensor_copy(picked[i][a][:], table[a][:].bitcast(U32).indirect(lists[i][:]))

        def quantize_chunk(key):
            b, a, i = key
            grouped = ring.tile([P, PACK * P * PACK], BF16, name="grouped", bufs=GROUPED_BUFS, align_bytes=64)
            dealt = grouped[:].rearrange("p (t m j) -> p m j t", t=PACK, j=PACK)
            span = P // len(raw[key])
            for n, part in enumerate(raw[key]):
                src = part.rearrange("p j (m t) -> p m j t", t=PACK)
                dst = dealt[:, n * span:(n + 1) * span]
                if (b > 0 and a == 0) or n == 1:
                    nc.vector.tensor_copy(out=dst, in_=src)
                else:
                    nc.scalar.copy(out=dst, in_=src)
            codes = ring.tile([P, KP], U32, name="codes", bufs=CODE_BUFS, align_bytes=64)
            plane = ring.tile([P, KP], U8, name="plane", bufs=CODE_BUFS, align_bytes=64)
            width = P if key == last_chunk else KP
            for c0 in range(0, KP, width):
                nc.vector.quantize_mx(out=codes[:, c0:c0 + width].bitcast(FP8X4), scales=plane[:, c0:c0 + width],
                                      in_=grouped[:, PACK * c0:PACK * (c0 + width)])
            quantised[key] = (codes, plane)

        def multiply(key, first, last):
            b, a, i = key
            if first:
                total[b] = [psum.tile([P, S], F32, name="bank%d" % (PACK * (b % 2) + t)) for t in range(PACK)]
            rhs_scale = (picked_plane, lowered_plane)[a][:, i * S:(i + 1) * S]
            for t in range(PACK):
                if i in weights:
                    codes, plane = quantised[key]
                    lhs = codes[:, t * P:(t + 1) * P].bitcast(FP8X4)
                    lhs_scale = plane[:, t * P:(t + 1) * P]
                else:
                    c0 = a * H + b * KP + t * P
                    lhs = w2_codes[:, 2 * c0:2 * (c0 + P)].bitcast(FP4X4)
                    lhs_scale = w2_plane[:, c0:c0 + P]
                nc.tensor.matmul_mx(out=total[b][t][:], lhsT=lhs, lhsT_scale=lhs_scale,
                                    rhs=picked[i][a][:].bitcast(FP8X4), rhs_scale=rhs_scale,
                                    start=first, stop=last)

        def bend(b):
            bent[b] = ring.tile([P, PACK, S], F32, name="bent", bufs=BENT_BUFS)
            for t in range(PACK):
                nc.scalar.activation(out=bent[b][:, t, :], in_=total[b][t][:], func=ACT.Tanh,
                                     bias=bias_sb[:, b, t:t + 1])
                nc.vector.scalar_tensor_tensor(out=bent[b][:, t, :], in0=bent[b][:, t, :],
                                               scalar=gain_sb[:, b, t:t + 1], in1=prof[b][:, t, :],
                                               op0=ALU.mult, op1=ALU.mult)

        def join(b, s0, width):
            cols = slice(s0, s0 + width)
            straight = ring.tile([P, PACK, width], F32, name="straight", bufs=JOIN_BUFS)
            for t in range(PACK):
                nc.scalar.activation(out=straight[:, t, :], in_=total[b][t][:, cols], func=ACT.Identity,
                                     bias=gain_bias[:, b, t:t + 1], scale=gain_sb[:, b, t:t + 1])
            h = ring.tile([P, width * PACK], BF16, name="h", bufs=JOIN_BUFS, align_bytes=64)
            nc.vector.tensor_tensor(out=h[:].rearrange("p (c e t) -> p c t e", e=RUN, t=PACK),
                                    in0=bent[b][:, :, cols].rearrange("p t (c e) -> p c t e", e=RUN),
                                    in1=straight[:].rearrange("p t (c e) -> p c t e", e=RUN), op=ALU.add)
            codes = held.tile([P, width], U32, name="h_codes%d_%d" % (b, s0), align_bytes=64)
            plane = held.tile([P, width], U8, name="h_plane%d_%d" % (b, s0), align_bytes=64)
            nc.vector.quantize_mx(out=codes[:].bitcast(FP8X4), scales=plane[:], in_=h[:])
            for c0 in range(0, width, PIECE):
                h_mx[(b, (s0 + c0) // PIECE)] = (codes[:, c0:c0 + PIECE], plane[:, c0:c0 + PIECE])

        def score(b, piece):
            if b == 0:
                scores[piece] = psum.tile([P, N // P, PIECE], F32, name="bank%d" % (PACK + piece))
            codes, plane = h_mx[(b, piece)]
            for m in range(N // P):
                c0 = b * N + m * P
                nc.tensor.matmul_mx(out=scores[piece][:, m, :],
                                    lhsT=w4_codes[:, c0:c0 + P].bitcast(FP8X4),
                                    lhsT_scale=w4_plane[W4_ROW:P, c0:c0 + P],
                                    rhs=codes.bitcast(FP8X4), rhs_scale=plane,
                                    start=(b == 0 and m == 0), stop=(b == BANDS - 1 and m == N // P - 1))

        def store(piece):
            staged = held.tile([P, N // P, PIECE], F32, name="staged%d" % piece)
            if piece == PIECES - 1:
                nc.vector.tensor_copy(out=staged[:], in_=scores[piece][:])
            else:
                nc.scalar.copy(out=staged[:], in_=scores[piece][:])
            dst = out[:, piece * PIECE:(piece + 1) * PIECE].rearrange("(m p) s -> p m s", p=P)
            nc.sync.dma_start(out=dst, in_=staged[:])

        nc.sync.dma_start(out=w2_raw[:].bitcast(I32).rearrange("p (a c) -> p a c", a=PASSES),
                          in_=w2_words.bitcast(I32).rearrange("a p c -> p a c"))
        for r in range(SCALE_ROWS):
            nc.sync.dma_start(out=tab_plane[r:P:LIFT, :].bitcast(I32),
                              in_=tab_scales[:, r::SCALE_ROWS, :].bitcast(I32).rearrange("a q c -> q a c"))
        nc.sync.dma_start(lists[0][:], offs)
        nc.sync.dma_start(lists[1][:], offs2)
        load_chunk(chunks[0])
        nc.sync.dma_start(lists[2][:], offs3)
        load_table(0)
        load_planes(w2_plane_raw, 0, w2_scales)
        load_chunk(chunks[1])

        nc.vector.tensor_copy(out=w2_codes[:].bitcast(U16).rearrange("p (g t m) -> p g t m", t=PACK, m=P),
                              in_=w2_raw[:].bitcast(U16).rearrange("p (g m t) -> p g t m", t=PACK, m=P))
        for i in range(LOOKUPS):
            nc.vector.tensor_copy(picked_plane[:, i * S:(i + 1) * S], tab_plane[:].indirect(lists[i][:]))
        for r in range(SCALE_ROWS):
            nc.sync.dma_start(out=lowered_plane[r:P:QUADRANT, :].bitcast(I32),
                              in_=picked_plane[LIFT + r:P:QUADRANT, :].bitcast(I32))

        load_chunk(chunks[2])
        load_table(1)
        nc.sync.dma_start(out=bias_sb[:, :, 0:PACK], in_=bias.rearrange("(b p t) -> p b t", p=P, t=PACK))
        nc.sync.dma_start(out=gain_sb[:, :, 0:PACK], in_=gain.rearrange("(b p t) -> p b t", p=P, t=PACK))
        for key in chunks[3:]:
            b, a, i = key
            load_chunk(key)
            if b > 0 and (a, i) == (0, 2):
                load_profile(b - 1)
            if key == (BANDS - 1, 0, 0):
                load_planes(w4_plane, W4_ROW, w4_scales)
        load_profile(BANDS - 1)
        w4_codes = ring.tile([P, BANDS * N], I32, name="stream", bufs=STREAM_BUFS, align_bytes=64)
        nc.sync.dma_start(out=w4_codes[:].rearrange("p (a c) -> p a c", a=BANDS),
                          in_=w4_words.rearrange("a p c i -> p a (c i)").bitcast(I32))

        quantize_chunk(chunks[0])
        gather_words(0)
        quantize_chunk(chunks[1])
        nc.vector.tensor_copy(out=w2_plane[:].rearrange("p (g t m) -> p g t m", t=PACK, m=P),
                              in_=w2_plane_raw[:].rearrange("p (g m t) -> p g t m", t=PACK, m=P))
        gather_words(1)
        nc.vector.tensor_tensor(out=gain_bias[:], in0=gain_sb[:, :, 0:PACK], in1=bias_sb[:, :, 0:PACK], op=ALU.mult)

        for b in range(BANDS):
            keys = [(b, a, i) for a in range(PASSES) for i in (1, 0, 2)]
            for key in keys:
                if key in raw and key not in quantised:
                    quantize_chunk(key)
                multiply(key, key == keys[0], key == keys[-1])
            if b < BANDS - 1:
                bend(b)
                join(b, 0, S)
        for b in range(BANDS - 1):
            for piece in range(PIECES):
                score(b, piece)
        bend(BANDS - 1)
        for piece in range(PIECES):
            join(BANDS - 1, piece * PIECE, PIECE)
        for piece in range(PIECES):
            score(BANDS - 1, piece)
            store(piece)
